import numpy as np
import ml_dtypes


def mxq(x, axis, fmt="e4m3"):
    dtype, down = {"e4m3": (ml_dtypes.float8_e4m3fn, 7), "e5m2": (ml_dtypes.float8_e5m2, 14)}[fmt]
    v = np.moveaxis(np.asarray(x, np.float32).astype(ml_dtypes.bfloat16).astype(np.float64), axis, -1)
    blocks = v.reshape(v.shape[:-1] + (-1, 32))
    amax = np.abs(blocks).max(-1, keepdims=True)
    byte = np.maximum(np.where(amax > 0, np.frexp(amax)[1] - 1 + 127, 0) - down, 1)
    scale = np.exp2(byte - 127.0)
    codes = (blocks / scale).astype(np.float32).astype(dtype).astype(np.float64)
    return np.moveaxis((codes * scale).reshape(v.shape), -1, axis)


WIDE = False


def mx_kscale(k):
    if not WIDE:
        return np.ones(k)
    levels = np.array([10, -10, 5, -5, 0])
    if k % 512:
        return np.exp2(np.random.permutation(np.resize(levels, k // 32))).repeat(32)
    a = np.empty((k // 512, 16))
    for p in range(k // 512):
        a[p, :8] = np.random.permutation(np.resize(levels, 8))
        for g in range(8):
            far = levels[np.abs(levels - a[p, g]) >= 10]
            a[p, g + 8] = far[np.random.randint(len(far))]
    return np.exp2(a.ravel()).repeat(32)


def f64(x):
    return np.asarray(x).astype(np.float64)


def striped(idx):
    return np.tile(idx.reshape(-1, 16).T, (8, 1)).astype(np.uint16)


def unstriped(offs):
    return offs[:16].T.reshape(-1).astype(np.int64)


E2M1 = np.array([0.0, 0.5, 1.0, 1.5, 2.0, 3.0, 4.0, 6.0, -0.0, -0.5, -1.0, -1.5, -2.0, -3.0, -4.0, -6.0])


def pack_weight(w, fmt):
    k, n = w.shape
    w = f64(np.asarray(w, np.float32).astype(ml_dtypes.bfloat16)).reshape(k // 32, 32, n)
    amax = np.abs(w).max(1)
    if fmt == "e4m3":
        byte = np.frexp(amax)[1] - 1 + 127 - 7
    else:
        mant, ex = np.frexp(amax / 6.0)
        byte = np.where(mant > 0.5, ex, ex - 1) + 127
    byte = np.clip(np.where(amax > 0, byte, 1), 1, 254)
    scaled = (w * np.exp2(127.0 - byte)[:, None, :]).reshape(k, n).astype(np.float32)
    by_word = np.ascontiguousarray(scaled.reshape(k // 512, 128, 4, n).transpose(0, 1, 3, 2))
    if fmt == "e4m3":
        words = by_word.astype(ml_dtypes.float8_e4m3fn).view(np.uint8)
    else:
        c = by_word.astype(ml_dtypes.float4_e2m1fn).view(np.uint8) & 0xF
        words = (c[..., 0::2] | (c[..., 1::2] << 4)).reshape(k // 512, 128, 2 * n)
    return np.ascontiguousarray(words), np.ascontiguousarray(byte.astype(np.uint8).reshape(k // 512, 16, n))


def unpack_weight(words, scales, fmt):
    g, _, n = scales.shape
    words = np.ascontiguousarray(words).reshape(g, 128, n, -1)
    if fmt == "e4m3":
        vals = words.view(ml_dtypes.float8_e4m3fn).astype(np.float64)
    else:
        nib = np.empty((g, 128, n, 4), np.uint8)
        nib[..., 0::2] = words & 0xF
        nib[..., 1::2] = words >> 4
        vals = E2M1[nib]
    vals = vals * np.repeat(np.exp2(scales.astype(np.float64) - 127.0), 8, axis=1)[..., None]
    return vals.transpose(0, 1, 3, 2).reshape(g * 512, n)


def gelu(v):
    return 0.5 * v * (1.0 + np.tanh(np.sqrt(2.0 / np.pi) * (v + 0.044715 * v**3)))


def striped8(idx):
    return np.concatenate([v.reshape(-1, 16).T for v in idx]).astype(np.uint16)


def unstriped8(offs):
    return np.stack([offs[16 * g:16 * g + 16].T.reshape(-1) for g in range(8)]).astype(np.int64)


def heads(h, wgt, idx8):
    r = np.arange(h.shape[0])
    return wgt[r // 4 % 128] * h[r[:, None], idx8[r % 512 // 64]]


def put_heads(h, wgs, idx8, t2):
    r = np.arange(h.shape[0])
    page = np.zeros((h.shape[0], t2))
    page[r[:, None], idx8[r % 512 // 64]] = wgs[r // 4 % 128] * h
    return page


T, S, P, T2, K, H, N = 4096, 1024, 1024, 2048, 1024, 1024, 384

def setup_inputs():
    n = np.random.standard_normal
    s = mx_kscale(K)[:, None]
    u = mx_kscale(H)[:, None]
    d = {}
    d["tab_words"], d["tab_scales"] = pack_weight(n((K, T)) * s, "e4m3")
    d["offs"] = striped(np.random.permutation(T)[:S])
    d["offs2"] = striped8(np.stack([np.random.permutation(T2)[:S] for _ in range(8)]))
    d["offs3"] = striped8(np.stack([np.random.permutation(T2)[:P] for _ in range(8)]))
    d["w1"] = (n((K, H)) / s * u.T / K ** 0.5).astype(np.float32)
    d["gain"] = np.exp(0.5 * n(H)).astype(np.float32)
    d["wgs"] = np.repeat(np.random.uniform(0.5, 2.0, (8, S)), 16, axis=0).astype(np.float32)
    d["wgt"] = np.repeat(np.random.uniform(0.5, 2.0, (8, P)), 16, axis=0).astype(np.float32)
    d["tinct"] = (n((H, P)) * u).astype(np.float32)
    d["w3"] = (n((K, N)) / s / K ** 0.5).astype(np.float32)
    d["w4_words"], d["w4_scales"] = pack_weight(0.7 * n((H, N)) / u / H ** 0.5, "e2m1")
    return d

def reference(tab_words, tab_scales, offs, offs2, offs3, w1, gain, wgs, wgt, tinct, w3, w4_words, w4_scales):
    v = unpack_weight(tab_words, tab_scales, "e4m3")[:, unstriped(offs)]
    w4 = unpack_weight(w4_words, w4_scales, "e2m1")
    h = f64(gain)[:, None] * (mxq(f64(w1), 0, "e4m3").T @ v)
    page = put_heads(h, f64(wgs), unstriped8(offs2), T2)
    x = heads(page, f64(wgt), unstriped8(offs3))
    z = x + f64(tinct)
    petition = w4.T @ mxq(z, 0, "e4m3")
    blazon = mxq(f64(w3), 0, "e4m3").T @ v
    diff = petition - blazon
    out = diff * diff
    return out

@@ -1,0 +1,326 @@
+from contextlib import ExitStack
+
+import concourse.mybir as mybir
+from concourse.masks import make_identity
+
+T, S, T2, K, H, N = 4096, 1024, 2048, 1024, 1024, 384
+FLOPS = 2 * S * (K * H + H * N + K * N)
+
+F32 = mybir.dt.float32
+BF16 = mybir.dt.bfloat16
+I32 = mybir.dt.int32
+U32 = mybir.dt.uint32
+U16 = mybir.dt.uint16
+U8 = mybir.dt.uint8
+FP8X4 = mybir.dt.float8_e4m3fn_x4
+FP4X4 = mybir.dt.float4_e2m1fn_x4
+MULT = mybir.AluOpType.mult
+ADD = mybir.AluOpType.add
+COPY = mybir.ActivationFunctionType.Copy
+SQUARE = mybir.ActivationFunctionType.Square
+
+P = 128
+PACK = 4
+K_PASS = P * PACK
+BANK = 512
+BLOCK = 128
+N_TILES = N // P
+BLOCKS = S // BLOCK
+LAG = 2
+DIRECT_BLOCKS = (3, 7)
+
+
+def tile_list_arms_conflict_scores_kernel(
+    tc, tab_words, tab_scales, offs, offs2, offs3, w1, gain, wgs, wgt, tinct, w3, w4_words, w4_scales, out
+):
+    nc = tc.nc
+
+    def entries(first, count):
+        return slice(first // 16, (first + count) // 16)
+
+    with ExitStack() as ctx:
+        lists = ctx.enter_context(tc.tile_pool(name="lists", bufs=1))
+        keep = ctx.enter_context(tc.tile_pool(name="keep", bufs=1))
+        ring = ctx.enter_context(tc.tile_pool(name="ring", bufs=3))
+        psum = ctx.enter_context(tc.psum_pool(name="psum", bufs=2))
+
+        idx = lists.tile([P, S // 16], U16, name="idx")
+        idx2 = lists.tile([P, S // 16], U16, name="idx2")
+        idx3 = lists.tile([P, S // 16], U16, name="idx3")
+
+        def kept(shape, dtype, name, tag=None):
+            return keep.tile(shape, dtype, name=name, tag=tag or name, align_bytes=64)
+
+        scale_rows = kept([P, T], U8, "scale_rows")
+        nc.vector.memset(scale_rows[:].bitcast(I32), 0)
+        for q in range(4):
+            nc.gpsimd.dma_start(
+                out=scale_rows[32 * q : 32 * q + 8, :].bitcast(I32),
+                in_=tab_scales[:, 4 * q : 4 * q + 4, :].bitcast(I32),
+            )
+        nc.sync.dma_start(idx[:], offs)
+
+        def load_w1(b, a):
+            raw = kept([P, PACK, K_PASS], F32, "w1_raw_%d%d" % (b, a), tag="w1_raw_%d" % a)
+            rows = w1[a * K_PASS : (a + 1) * K_PASS, b * K_PASS : (b + 1) * K_PASS]
+            nc.sync.dma_start(out=raw[:], in_=rows.rearrange("(p j) c -> p j c", j=PACK))
+            return raw
+
+        def group_w1(raw, dst):
+            nc.scalar.copy(
+                out=dst.rearrange("p (t m j) -> p m t j", t=PACK, j=PACK),
+                in_=raw[:].rearrange("p j (m t) -> p m t j", t=PACK),
+            )
+
+        w1_raw = [load_w1(0, a) for a in range(2)]
+        words = []
+        for a in range(2):
+            table = kept([P, T], I32, "table_%d" % a, tag="big_%d" % a)
+            nc.sync.dma_start(out=table[:], in_=tab_words[a].rearrange("p t i -> p (t i)").bitcast(I32))
+            words.append(table)
+
+        gains = kept([P, 2 * PACK], F32, "gains")
+        nc.sync.dma_start(
+            out=gains[:].rearrange("p (b i) -> p b i", b=2), in_=gain.rearrange("(b p i) -> p b i", b=2, i=PACK)
+        )
+        nc.sync.dma_start(idx2[:], offs2)
+        wgs_sb = kept([P, S], F32, "wgs_sb")
+        nc.sync.dma_start(out=wgs_sb[:], in_=wgs)
+        nc.sync.dma_start(idx3[:], offs3)
+        wgt_sb = kept([P, S], F32, "wgt_sb")
+        nc.sync.dma_start(out=wgt_sb[:], in_=wgt)
+
+        v_scales = kept([P, S], U8, "v_scales")
+        nc.vector.tensor_copy(v_scales[:], scale_rows[:].indirect(idx[:]))
+
+        pages = [kept([P, T2], F32, "page_%d" % i) for i in range(PACK)]
+        for page in pages:
+            nc.vector.memset(page[:], 0.0)
+
+        identity = kept([P, P], F32, "identity")
+        make_identity(nc, identity[:])
+
+        w1_codes = [kept([P, 2 * K_PASS], I32, "w1_codes_%d" % b) for b in range(2)]
+        w1_scales = [kept([P, 2 * K_PASS], U8, "w1_scales_%d" % b) for b in range(2)]
+        for a in range(2):
+            grouped = kept([P, PACK * K_PASS], BF16, "w1_grouped_%d" % a, tag="x_%d" % a)
+            group_w1(w1_raw[a], grouped[:])
+            cols = slice(a * K_PASS, (a + 1) * K_PASS)
+            nc.vector.quantize_mx(out=w1_codes[0][:, cols].bitcast(FP8X4), scales=w1_scales[0][:, cols], in_=grouped[:])
+
+        v_codes = [kept([P, S], I32, "v_codes_0", tag="scale_rows"), kept([P, S], I32, "v_codes_1")]
+        nc.vector.tensor_copy(v_codes[0][:].bitcast(U32), words[0][:].bitcast(U32).indirect(idx[:]))
+        for first in range(0, S, BANK):
+            nc.vector.tensor_copy(
+                v_codes[1][:, first : first + BANK].bitcast(U32),
+                words[1][:].bitcast(U32).indirect(idx[:, entries(first, BANK)]),
+            )
+
+        def features(b, i):
+            h = kept([P, S], F32, "h_%d%d" % (b, i), tag="h_%d" % i)
+            banks = [psum.tile([P, BANK], F32, name="h_bank", tag="h_bank") for half in range(2)]
+            for a in range(2):
+                w_cols = slice(a * K_PASS + i * P, a * K_PASS + (i + 1) * P)
+                for half in range(2):
+                    cols = slice(half * BANK, (half + 1) * BANK)
+                    nc.tensor.matmul_mx(
+                        out=banks[half][:],
+                        lhsT=w1_codes[b][:, w_cols].bitcast(FP8X4),
+                        lhsT_scale=w1_scales[b][:, w_cols],
+                        rhs=v_codes[a][:, cols].bitcast(FP8X4),
+                        rhs_scale=v_scales[4 * a : P, cols],
+                        start=(a == 0),
+                        stop=(a == 1),
+                    )
+            for half in range(2):
+                cols = slice(half * BANK, (half + 1) * BANK)
+                nc.scalar.activation(
+                    out=h[:, cols], in_=banks[half][:], func=COPY, scale=gains[:, PACK * b + i : PACK * b + i + 1]
+                )
+            return h
+
+        def file_entries(h, i, first, count):
+            cols = slice(first, first + count)
+            nc.vector.tensor_tensor(
+                pages[i][:].indirect(idx2[:, entries(first, count)]), h[:, cols], wgs_sb[:, cols], MULT
+            )
+
+        def read_entries(x, i, first, count):
+            nc.vector.tensor_tensor(
+                x, pages[i][:].indirect(idx3[:, entries(first, count)]), wgt_sb[:, first : first + count], MULT
+            )
+
+        h_first = [features(0, i) for i in range(PACK)]
+
+        w1_raw = [load_w1(1, a) for a in range(2)]
+        tinct_sb = []
+        for b in range(2):
+            rows = kept([P, PACK, S], F32, "tinct_%d" % b, tag="big_%d" % b)
+            tinct_sb.append(rows)
+
+        def load_tinct(b):
+            nc.sync.dma_start(
+                out=tinct_sb[b][:], in_=tinct[b * K_PASS : (b + 1) * K_PASS, :].rearrange("(p i) j -> p i j", i=PACK)
+            )
+
+        load_tinct(0)
+        w3_raw = []
+        for a in range(2):
+            raw = kept([P, PACK, N], F32, "w3_raw_%d" % a)
+            nc.sync.dma_start(
+                out=raw[:], in_=w3[a * K_PASS : (a + 1) * K_PASS, :].rearrange("(p j) c -> p j c", j=PACK)
+            )
+            w3_raw.append(raw)
+        w4_codes = kept([P, 2, 2 * N], U8, "w4_codes")
+        nc.sync.dma_start(out=w4_codes[:].bitcast(I32), in_=w4_words.rearrange("a p n -> p a n").bitcast(I32))
+        w4_planes = kept([P, 2, N], U8, "w4_planes")
+        nc.vector.memset(w4_planes[:].bitcast(I32), 0)
+        for q in range(4):
+            nc.sync.dma_start(
+                out=w4_planes[32 * q : 32 * q + 4].bitcast(I32),
+                in_=w4_scales[:, 4 * q : 4 * q + 4, :].rearrange("a r n -> r a n").bitcast(I32),
+            )
+        load_tinct(1)
+
+        grouped = kept([P, 2 * PACK * K_PASS], BF16, "w1_grouped_late", tag="x_23")
+        for a in range(2):
+            group_w1(w1_raw[a], grouped[:, a * PACK * K_PASS : (a + 1) * PACK * K_PASS])
+        nc.vector.quantize_mx(out=w1_codes[1][:].bitcast(FP8X4), scales=w1_scales[1][:], in_=grouped[:])
+
+        x_01 = [kept([P, S], F32, "x_%d" % i) for i in range(2)]
+        x_23 = kept([P, 2 * S], F32, "x_23")
+        x_first = [x_01[0][:], x_01[1][:], x_23[:, 0:S], x_23[:, S : 2 * S]]
+        for first in range(0, S, BANK):
+            file_entries(h_first[0], 0, first, BANK)
+        for i in range(1, PACK):
+            file_entries(h_first[i], i, 0, S)
+            read_entries(x_first[i - 1], i - 1, 0, S)
+        read_entries(x_first[PACK - 1], PACK - 1, 0, S)
+
+        h_second = [features(1, i) for i in range(PACK)]
+        for i in range(PACK):
+            file_entries(h_second[i], i, 0, S)
+
+        def add_and_group(b, c, x_rows, dst):
+            cols = slice(c * BLOCK, (c + 1) * BLOCK)
+            z_t = psum.tile([P, PACK, P], F32, name="z_t", tag="z_t")
+            for i in range(PACK):
+                nc.tensor.matmul(
+                    z_t[:, i, :], tinct_sb[b][:, i, cols], identity[:], start=(i == 0), stop=False, is_transpose=True
+                )
+            for i in range(PACK):
+                nc.tensor.matmul(
+                    z_t[:, i, :], x_rows[i], identity[:], start=False, stop=(i == PACK - 1), is_transpose=True
+                )
+            pairs = ring.tile([P, PACK * P], BF16, name="pairs", tag="pairs", align_bytes=64)
+            nc.scalar.copy(
+                out=pairs[:].rearrange("j (u p e) -> j u p e", u=2, e=2),
+                in_=z_t[:].rearrange("j (u e) p -> j u p e", u=2),
+            )
+            back = psum.tile([P, 2, BLOCK], F32, name="back", tag="back")
+            for u in range(2):
+                nc.tensor.transpose(back[:, u, :], pairs[:].bitcast(F32)[:, u * P : (u + 1) * P], identity[:])
+            nc.scalar.copy(
+                out=dst.bitcast(F32).rearrange("p (j u) -> p j u", u=2), in_=back[:].rearrange("p u j -> p j u")
+            )
+
+        z0_grouped = [kept([P, PACK * BANK], BF16, "z0_grouped_%d" % half) for half in range(2)]
+        for half in range(2):
+            grouped = z0_grouped[half]
+            for c in range(4 * half, 4 * half + 4):
+                cols = slice(c * BLOCK, (c + 1) * BLOCK)
+                local = c - 4 * half
+                add_and_group(
+                    0, c, [x[:, cols] for x in x_first], grouped[:, local * PACK * BLOCK : (local + 1) * PACK * BLOCK]
+                )
+        z0_codes = kept([P, S], I32, "z0_codes", tag="h_3")
+        z0_scales = kept([P, S], U8, "z0_scales")
+
+        def quantize_z0(half):
+            cols = slice(half * BANK, (half + 1) * BANK)
+            nc.vector.quantize_mx(
+                out=z0_codes[:, cols].bitcast(FP8X4), scales=z0_scales[:, cols], in_=z0_grouped[half][:]
+            )
+
+        w3_grouped = kept([P, 2 * N * PACK], BF16, "w3_grouped")
+        for a in range(2):
+            nc.scalar.activation(
+                out=w3_grouped[:, a * N * PACK : (a + 1) * N * PACK].rearrange("p (c j) -> p c j", j=PACK),
+                in_=w3_raw[a][:].rearrange("p j c -> p c j"),
+                func=COPY,
+                scale=-1.0,
+            )
+        w3_codes = kept([P, 2 * N], I32, "w3_codes", tag="h_2")
+        w3_scales = kept([P, 2 * N], U8, "w3_scales")
+
+        def quantize_w3():
+            for lo, hi in ((0, 512), (512, 2 * N)):
+                nc.vector.quantize_mx(
+                    out=w3_codes[:, lo:hi].bitcast(FP8X4),
+                    scales=w3_scales[:, lo:hi],
+                    in_=w3_grouped[:, PACK * lo : PACK * hi],
+                )
+
+        def scores(c, z1_codes, z1_scales):
+            cols = slice(c * BLOCK, (c + 1) * BLOCK)
+            tag = "h_bank" if c % 2 else "diff"
+            diff = psum.tile([P, N_TILES, BLOCK], F32, name="diff", tag=tag)
+            for a in range(2):
+                for t in range(N_TILES):
+                    w_cols = slice(a * N + t * P, a * N + (t + 1) * P)
+                    nc.tensor.matmul_mx(
+                        out=diff[:, t, :],
+                        lhsT=w3_codes[:, w_cols].bitcast(FP8X4),
+                        lhsT_scale=w3_scales[:, w_cols],
+                        rhs=v_codes[a][:, cols].bitcast(FP8X4),
+                        rhs_scale=v_scales[4 * a : P, cols],
+                        start=(a == 0 and t == 0),
+                        stop=False,
+                    )
+            z_parts = [(z0_codes[:, cols], z0_scales[:, cols]), (z1_codes[:], z1_scales[:])]
+            for b in range(2):
+                for t in range(N_TILES):
+                    nc.tensor.matmul_mx(
+                        out=diff[:, t, :],
+                        lhsT=w4_codes[:, b, 2 * t * P : 2 * (t + 1) * P].bitcast(FP4X4),
+                        lhsT_scale=w4_planes[:, b, t * P : (t + 1) * P],
+                        rhs=z_parts[b][0].bitcast(FP8X4),
+                        rhs_scale=z_parts[b][1],
+                        start=False,
+                        stop=(b == 1 and t == N_TILES - 1),
+                    )
+            squared = ring.tile([P, N_TILES, BLOCK], F32, name="squared", tag="squared")
+            nc.scalar.activation(out=squared[:], in_=diff[:], func=SQUARE)
+            nc.sync.dma_start(out=out[:, cols].rearrange("(t p) j -> p t j", p=P), in_=squared[:])
+
+        z1_grouped = []
+        for step in range(BLOCKS + LAG):
+            if step < BLOCKS:
+                c = step
+                slot = "late_%d" % (c % (LAG + 1))
+                x = kept([P, PACK, BLOCK], F32, "x_late_%d" % c, tag=slot)
+                for i in range(PACK):
+                    read_entries(x[:, i, :], i, c * BLOCK, BLOCK)
+                if c in DIRECT_BLOCKS:
+                    grouped = kept([P, PACK * BLOCK], BF16, "z1_direct_%d" % c)
+                    nc.vector.tensor_tensor(
+                        grouped[:].rearrange("p (j i) -> p j i", i=PACK),
+                        x[:].rearrange("p i j -> p j i"),
+                        tinct_sb[1][:, :, c * BLOCK : (c + 1) * BLOCK].rearrange("p i j -> p j i"),
+                        ADD,
+                    )
+                else:
+                    grouped = kept([P, PACK * BLOCK], BF16, "z1_grouped_%d" % c, tag=slot)
+                    add_and_group(1, c, [x[:, i, :] for i in range(PACK)], grouped[:])
+                z1_grouped.append(grouped)
+            if step == 1:
+                quantize_w3()
+                quantize_z0(0)
+            if step == 3:
+                quantize_z0(1)
+            if step >= LAG:
+                c = step - LAG
+                z1_codes = ring.tile([P, BLOCK], I32, name="z1_codes", tag="z1_codes", align_bytes=64)
+                z1_scales = ring.tile([P, BLOCK], U8, name="z1_scales", tag="z1_scales", align_bytes=64)
+                nc.vector.quantize_mx(out=z1_codes[:].bitcast(FP8X4), scales=z1_scales[:], in_=z1_grouped[c][:])
+                scores(c, z1_codes, z1_scales)

@@ -53,11 +53,6 @@ def tile_list_arms_conflict_scores_kernel(
 
         scale_rows = kept([P, T], U8, "scale_rows")
         nc.vector.memset(scale_rows[:].bitcast(I32), 0)
-        for q in range(4):
-            nc.gpsimd.dma_start(
-                out=scale_rows[32 * q : 32 * q + 8, :].bitcast(I32),
-                in_=tab_scales[:, 4 * q : 4 * q + 4, :].bitcast(I32),
-            )
         nc.sync.dma_start(idx[:], offs)
 
         def load_w1(b, a):
@@ -66,18 +61,25 @@ def tile_list_arms_conflict_scores_kernel(
             nc.sync.dma_start(out=raw[:], in_=rows.rearrange("(p j) c -> p j c", j=PACK))
             return raw
 
-        def group_w1(raw, dst):
-            nc.scalar.copy(
-                out=dst.rearrange("p (t m j) -> p m t j", t=PACK, j=PACK),
-                in_=raw[:].rearrange("p j (m t) -> p m t j", t=PACK),
+        def group_w1(copy_call, raw, dst):
+            copy_call(
+                out=dst.rearrange("p (t m j) -> p t m j", t=PACK, j=PACK),
+                in_=raw[:].rearrange("p j (m t) -> p t m j", t=PACK),
             )
 
-        w1_raw = [load_w1(0, a) for a in range(2)]
-        words = []
-        for a in range(2):
+        def load_words(a):
             table = kept([P, T], I32, "table_%d" % a, tag="big_%d" % a)
             nc.sync.dma_start(out=table[:], in_=tab_words[a].rearrange("p t i -> p (t i)").bitcast(I32))
-            words.append(table)
+            return table
+
+        words = [load_words(0)]
+        for q in range(4):
+            nc.sync.dma_start(
+                out=scale_rows[32 * q : 32 * q + 8, :].bitcast(I32),
+                in_=tab_scales[:, 4 * q : 4 * q + 4, :].bitcast(I32),
+            )
+        w1_raw = [load_w1(0, a) for a in range(2)]
+        words.append(load_words(1))
 
         gains = kept([P, 2 * PACK], F32, "gains")
         nc.sync.dma_start(
@@ -90,26 +92,33 @@ def tile_list_arms_conflict_scores_kernel(
         wgt_sb = kept([P, S], F32, "wgt_sb")
         nc.sync.dma_start(out=wgt_sb[:], in_=wgt)
 
+        v_codes = [kept([P, S], I32, "v_codes_0")]
+        nc.vector.tensor_copy(v_codes[0][:].bitcast(U32), words[0][:].bitcast(U32).indirect(idx[:]))
         v_scales = kept([P, S], U8, "v_scales")
         nc.vector.tensor_copy(v_scales[:], scale_rows[:].indirect(idx[:]))
 
         pages = [kept([P, T2], F32, "page_%d" % i) for i in range(PACK)]
-        for page in pages:
-            nc.vector.memset(page[:], 0.0)
+        nc.vector.memset(pages[0][:], 0.0)
+        for page in pages[1:]:
+            nc.gpsimd.memset(page[:], 0.0)
 
         identity = kept([P, P], F32, "identity")
         make_identity(nc, identity[:])
 
         w1_codes = [kept([P, 2 * K_PASS], I32, "w1_codes_%d" % b) for b in range(2)]
-        w1_scales = [kept([P, 2 * K_PASS], U8, "w1_scales_%d" % b) for b in range(2)]
+        early_planes = kept([P, K_PASS], U8, "w1_early_planes")
+        late_planes = kept([P, 2 * K_PASS], U8, "w1_late_planes")
+        w1_planes = [
+            [early_planes[4 * a : P, :] for a in range(2)],
+            [late_planes[:, a * K_PASS : (a + 1) * K_PASS] for a in range(2)],
+        ]
         for a in range(2):
-            grouped = kept([P, PACK * K_PASS], BF16, "w1_grouped_%d" % a, tag="x_%d" % a)
-            group_w1(w1_raw[a], grouped[:])
+            grouped = kept([P, PACK * K_PASS], BF16, "w1_grouped_%d" % a, tag=("w1_grouped_0", "scale_rows")[a])
+            group_w1((nc.scalar.copy, nc.vector.tensor_copy)[a], w1_raw[a], grouped[:])
             cols = slice(a * K_PASS, (a + 1) * K_PASS)
-            nc.vector.quantize_mx(out=w1_codes[0][:, cols].bitcast(FP8X4), scales=w1_scales[0][:, cols], in_=grouped[:])
+            nc.vector.quantize_mx(out=w1_codes[0][:, cols].bitcast(FP8X4), scales=w1_planes[0][a], in_=grouped[:])
 
-        v_codes = [kept([P, S], I32, "v_codes_0", tag="scale_rows"), kept([P, S], I32, "v_codes_1")]
-        nc.vector.tensor_copy(v_codes[0][:].bitcast(U32), words[0][:].bitcast(U32).indirect(idx[:]))
+        v_codes.append(kept([P, S], I32, "v_codes_1", tag="scale_rows"))
         for first in range(0, S, BANK):
             nc.vector.tensor_copy(
                 v_codes[1][:, first : first + BANK].bitcast(U32),
@@ -126,7 +135,7 @@ def tile_list_arms_conflict_scores_kernel(
                     nc.tensor.matmul_mx(
                         out=banks[half][:],
                         lhsT=w1_codes[b][:, w_cols].bitcast(FP8X4),
-                        lhsT_scale=w1_scales[b][:, w_cols],
+                        lhsT_scale=w1_planes[b][a][:, i * P : (i + 1) * P],
                         rhs=v_codes[a][:, cols].bitcast(FP8X4),
                         rhs_scale=v_scales[4 * a : P, cols],
                         start=(a == 0),
@@ -182,20 +191,19 @@ def tile_list_arms_conflict_scores_kernel(
             )
         load_tinct(1)
 
-        grouped = kept([P, 2 * PACK * K_PASS], BF16, "w1_grouped_late", tag="x_23")
+        grouped = kept([P, 2 * PACK * K_PASS], BF16, "w1_grouped_late", tag="x_first")
         for a in range(2):
-            group_w1(w1_raw[a], grouped[:, a * PACK * K_PASS : (a + 1) * PACK * K_PASS])
-        nc.vector.quantize_mx(out=w1_codes[1][:].bitcast(FP8X4), scales=w1_scales[1][:], in_=grouped[:])
+            group_w1(nc.scalar.copy, w1_raw[a], grouped[:, a * PACK * K_PASS : (a + 1) * PACK * K_PASS])
+        nc.vector.quantize_mx(out=w1_codes[1][:].bitcast(FP8X4), scales=late_planes[:], in_=grouped[:])
 
-        x_01 = [kept([P, S], F32, "x_%d" % i) for i in range(2)]
-        x_23 = kept([P, 2 * S], F32, "x_23")
-        x_first = [x_01[0][:], x_01[1][:], x_23[:, 0:S], x_23[:, S : 2 * S]]
+        x_rows_first = kept([P, PACK * S], F32, "x_first")
+        x_first = [x_rows_first[:, i * S : (i + 1) * S] for i in range(PACK)]
         for first in range(0, S, BANK):
             file_entries(h_first[0], 0, first, BANK)
         for i in range(1, PACK):
             file_entries(h_first[i], i, 0, S)
-            read_entries(x_first[i - 1], i - 1, 0, S)
-        read_entries(x_first[PACK - 1], PACK - 1, 0, S)
+        for i in range(PACK):
+            read_entries(x_first[i], i, 0, S)
 
         h_second = [features(1, i) for i in range(PACK)]
         for i in range(PACK):
@@ -303,11 +311,11 @@ def tile_list_arms_conflict_scores_kernel(
                     read_entries(x[:, i, :], i, c * BLOCK, BLOCK)
                 if c in DIRECT_BLOCKS:
                     grouped = kept([P, PACK * BLOCK], BF16, "z1_direct_%d" % c)
-                    nc.vector.tensor_tensor(
-                        grouped[:].rearrange("p (j i) -> p j i", i=PACK),
-                        x[:].rearrange("p i j -> p j i"),
-                        tinct_sb[1][:, :, c * BLOCK : (c + 1) * BLOCK].rearrange("p i j -> p j i"),
-                        ADD,
+                    rounded = kept([P, PACK, BLOCK], BF16, "z1_rounded_%d" % c)
+                    nc.vector.tensor_tensor(rounded[:], x[:], tinct_sb[1][:, :, c * BLOCK : (c + 1) * BLOCK], ADD)
+                    copy_call = nc.vector.tensor_copy if c == BLOCKS - 1 else nc.scalar.copy
+                    copy_call(
+                        out=grouped[:].rearrange("p (j i) -> p j i", i=PACK), in_=rounded[:].rearrange("p i j -> p j i")
                     )
                 else:
                     grouped = kept([P, PACK * BLOCK], BF16, "z1_grouped_%d" % c, tag=slot)

@@ -27,7 +27,7 @@ BLOCK = 128
 N_TILES = N // P
 BLOCKS = S // BLOCK
 LAG = 2
-DIRECT_BLOCKS = (3, 7)
+ROUTED = 4
 
 
 def tile_list_arms_conflict_scores_kernel(
@@ -42,21 +42,20 @@ def tile_list_arms_conflict_scores_kernel(
         lists = ctx.enter_context(tc.tile_pool(name="lists", bufs=1))
         keep = ctx.enter_context(tc.tile_pool(name="keep", bufs=1))
         ring = ctx.enter_context(tc.tile_pool(name="ring", bufs=3))
-        psum = ctx.enter_context(tc.psum_pool(name="psum", bufs=2))
+        psum = ctx.enter_context(tc.psum_pool(name="psum", bufs=1))
 
         idx = lists.tile([P, S // 16], U16, name="idx")
         idx2 = lists.tile([P, S // 16], U16, name="idx2")
         idx3 = lists.tile([P, S // 16], U16, name="idx3")
 
-        def kept(shape, dtype, name, tag=None):
-            return keep.tile(shape, dtype, name=name, tag=tag or name, align_bytes=64)
+        def kept(shape, dtype, name, tag=None, pool=keep):
+            return pool.tile(shape, dtype, name=name, tag=tag or name, align_bytes=64)
 
-        scale_rows = kept([P, T], U8, "scale_rows")
-        nc.vector.memset(scale_rows[:].bitcast(I32), 0)
-        nc.sync.dma_start(idx[:], offs)
+        def bank(n, shape, name):
+            return psum.tile(shape, F32, name=name, tag="bank_%d" % n)
 
-        def load_w1(b, a):
-            raw = kept([P, PACK, K_PASS], F32, "w1_raw_%d%d" % (b, a), tag="w1_raw_%d" % a)
+        def load_w1(b, a, pool):
+            raw = kept([P, PACK, K_PASS], F32, "w1_raw_%d%d" % (b, a), pool=pool)
             rows = w1[a * K_PASS : (a + 1) * K_PASS, b * K_PASS : (b + 1) * K_PASS]
             nc.sync.dma_start(out=raw[:], in_=rows.rearrange("(p j) c -> p j c", j=PACK))
             return raw
@@ -67,40 +66,55 @@ def tile_list_arms_conflict_scores_kernel(
                 in_=raw[:].rearrange("p j (m t) -> p t m j", t=PACK),
             )
 
-        def load_words(a):
-            table = kept([P, T], I32, "table_%d" % a, tag="big_%d" % a)
+        def load_words(a, pool):
+            table = kept([P, T], I32, "table_%d" % a, tag="big_%d" % a, pool=pool)
             nc.sync.dma_start(out=table[:], in_=tab_words[a].rearrange("p t i -> p (t i)").bitcast(I32))
             return table
 
-        words = [load_words(0)]
-        for q in range(4):
+        picked_rows = kept([P, S], U8, "picked_rows")
+        v_scales = [kept([P, S], U8, "v_scales_%d" % a) for a in range(2)]
+        with tc.tile_pool(name="scale_stage", bufs=1) as scale_stage:
+            scale_rows = kept([P, T], U8, "scale_rows", pool=scale_stage)
             nc.sync.dma_start(
-                out=scale_rows[32 * q : 32 * q + 8, :].bitcast(I32),
-                in_=tab_scales[:, 4 * q : 4 * q + 4, :].bitcast(I32),
+                out=scale_rows[0:32, :].bitcast(I32), in_=tab_scales.rearrange("a q t -> (a q) t").bitcast(I32)
             )
-        w1_raw = [load_w1(0, a) for a in range(2)]
-        words.append(load_words(1))
+            nc.gpsimd.memset(scale_rows[32:64, :].bitcast(I32), 0)
+            nc.gpsimd.memset(scale_rows[64:128, :].bitcast(I32), 0)
+            for plane in v_scales:
+                nc.vector.memset(plane[:].bitcast(I32), 0)
+            nc.sync.dma_start(idx[:], offs)
+            words = [load_words(0, keep)]
+            nc.sync.dma_start(idx2[:], offs2)
+            nc.sync.dma_start(idx3[:], offs3)
+            w1_raw = [load_w1(0, a, keep) for a in range(2)]
+            nc.vector.tensor_copy(picked_rows[:], scale_rows[:].indirect(idx[:]))
+        late = ctx.enter_context(tc.tile_pool(name="late", bufs=1))
 
-        gains = kept([P, 2 * PACK], F32, "gains")
+        def place_scale_rows(a):
+            for q in range(4):
+                nc.sync.dma_start(
+                    out=v_scales[a][32 * q : 32 * q + 4, :].bitcast(I32),
+                    in_=picked_rows[16 * a + 4 * q : 16 * a + 4 * q + 4, :].bitcast(I32),
+                )
+
+        place_scale_rows(0)
+        words.append(load_words(1, late))
+        place_scale_rows(1)
+        gains = kept([P, 2 * PACK], F32, "gains", pool=late)
         nc.sync.dma_start(
             out=gains[:].rearrange("p (b i) -> p b i", b=2), in_=gain.rearrange("(b p i) -> p b i", b=2, i=PACK)
         )
-        nc.sync.dma_start(idx2[:], offs2)
-        wgs_sb = kept([P, S], F32, "wgs_sb")
+        wgs_sb = kept([P, S], F32, "wgs_sb", pool=late)
         nc.sync.dma_start(out=wgs_sb[:], in_=wgs)
-        nc.sync.dma_start(idx3[:], offs3)
-        wgt_sb = kept([P, S], F32, "wgt_sb")
+        wgt_sb = kept([P, S], F32, "wgt_sb", pool=late)
         nc.sync.dma_start(out=wgt_sb[:], in_=wgt)
 
         v_codes = [kept([P, S], I32, "v_codes_0")]
         nc.vector.tensor_copy(v_codes[0][:].bitcast(U32), words[0][:].bitcast(U32).indirect(idx[:]))
-        v_scales = kept([P, S], U8, "v_scales")
-        nc.vector.tensor_copy(v_scales[:], scale_rows[:].indirect(idx[:]))
 
-        pages = [kept([P, T2], F32, "page_%d" % i) for i in range(PACK)]
+        pages = [kept([P, T2], F32, "page_%d" % i) for i in range(2)]
         nc.vector.memset(pages[0][:], 0.0)
-        for page in pages[1:]:
-            nc.gpsimd.memset(page[:], 0.0)
+        nc.gpsimd.memset(pages[1][:], 0.0)
 
         identity = kept([P, P], F32, "identity")
         make_identity(nc, identity[:])
@@ -113,12 +127,12 @@ def tile_list_arms_conflict_scores_kernel(
             [late_planes[:, a * K_PASS : (a + 1) * K_PASS] for a in range(2)],
         ]
         for a in range(2):
-            grouped = kept([P, PACK * K_PASS], BF16, "w1_grouped_%d" % a, tag=("w1_grouped_0", "scale_rows")[a])
+            grouped = kept([P, PACK * K_PASS], BF16, "w1_grouped_%d" % a, tag="w1_grouped_%d" % a, pool=(keep, late)[a])
             group_w1((nc.scalar.copy, nc.vector.tensor_copy)[a], w1_raw[a], grouped[:])
             cols = slice(a * K_PASS, (a + 1) * K_PASS)
             nc.vector.quantize_mx(out=w1_codes[0][:, cols].bitcast(FP8X4), scales=w1_planes[0][a], in_=grouped[:])
 
-        v_codes.append(kept([P, S], I32, "v_codes_1", tag="scale_rows"))
+        v_codes.append(kept([P, S], I32, "v_codes_1", tag="w1_grouped_1", pool=late))
         for first in range(0, S, BANK):
             nc.vector.tensor_copy(
                 v_codes[1][:, first : first + BANK].bitcast(U32),
@@ -127,7 +141,7 @@ def tile_list_arms_conflict_scores_kernel(
 
         def features(b, i):
             h = kept([P, S], F32, "h_%d%d" % (b, i), tag="h_%d" % i)
-            banks = [psum.tile([P, BANK], F32, name="h_bank", tag="h_bank") for half in range(2)]
+            banks = [bank(half, [P, BANK], "h_bank") for half in range(2)]
             for a in range(2):
                 w_cols = slice(a * K_PASS + i * P, a * K_PASS + (i + 1) * P)
                 for half in range(2):
@@ -137,7 +151,7 @@ def tile_list_arms_conflict_scores_kernel(
                         lhsT=w1_codes[b][:, w_cols].bitcast(FP8X4),
                         lhsT_scale=w1_planes[b][a][:, i * P : (i + 1) * P],
                         rhs=v_codes[a][:, cols].bitcast(FP8X4),
-                        rhs_scale=v_scales[4 * a : P, cols],
+                        rhs_scale=v_scales[a][:, cols],
                         start=(a == 0),
                         stop=(a == 1),
                     )
@@ -161,28 +175,25 @@ def tile_list_arms_conflict_scores_kernel(
 
         h_first = [features(0, i) for i in range(PACK)]
 
-        w1_raw = [load_w1(1, a) for a in range(2)]
-        tinct_sb = []
-        for b in range(2):
-            rows = kept([P, PACK, S], F32, "tinct_%d" % b, tag="big_%d" % b)
-            tinct_sb.append(rows)
+        w1_raw = [load_w1(1, a, late) for a in range(2)]
+        tinct_sb = [kept([P, PACK, S], F32, "tinct_0", tag="big_0"), kept([P, PACK, S], F32, "tinct_1", pool=late)]
 
         def load_tinct(b):
             nc.sync.dma_start(
                 out=tinct_sb[b][:], in_=tinct[b * K_PASS : (b + 1) * K_PASS, :].rearrange("(p i) j -> p i j", i=PACK)
             )
 
-        load_tinct(0)
         w3_raw = []
         for a in range(2):
-            raw = kept([P, PACK, N], F32, "w3_raw_%d" % a)
+            raw = kept([P, PACK, N], F32, "w3_raw_%d" % a, pool=late)
             nc.sync.dma_start(
                 out=raw[:], in_=w3[a * K_PASS : (a + 1) * K_PASS, :].rearrange("(p j) c -> p j c", j=PACK)
             )
             w3_raw.append(raw)
-        w4_codes = kept([P, 2, 2 * N], U8, "w4_codes")
+        load_tinct(0)
+        w4_codes = kept([P, 2, 2 * N], U8, "w4_codes", pool=late)
         nc.sync.dma_start(out=w4_codes[:].bitcast(I32), in_=w4_words.rearrange("a p n -> p a n").bitcast(I32))
-        w4_planes = kept([P, 2, N], U8, "w4_planes")
+        w4_planes = kept([P, 2, N], U8, "w4_planes", pool=late)
         nc.vector.memset(w4_planes[:].bitcast(I32), 0)
         for q in range(4):
             nc.sync.dma_start(
@@ -191,10 +202,34 @@ def tile_list_arms_conflict_scores_kernel(
             )
         load_tinct(1)
 
-        grouped = kept([P, 2 * PACK * K_PASS], BF16, "w1_grouped_late", tag="x_first")
+        late_grouped = kept([P, 2 * PACK * (K_PASS + N)], BF16, "late_grouped", tag="x_first")
         for a in range(2):
-            group_w1(nc.scalar.copy, w1_raw[a], grouped[:, a * PACK * K_PASS : (a + 1) * PACK * K_PASS])
-        nc.vector.quantize_mx(out=w1_codes[1][:].bitcast(FP8X4), scales=late_planes[:], in_=grouped[:])
+            group_w1(nc.scalar.copy, w1_raw[a], late_grouped[:, a * PACK * K_PASS : (a + 1) * PACK * K_PASS])
+        nc.vector.quantize_mx(
+            out=w1_codes[1][:].bitcast(FP8X4), scales=late_planes[:], in_=late_grouped[:, 0 : 2 * PACK * K_PASS]
+        )
+
+        w3_grouped = late_grouped[:, 2 * PACK * K_PASS :]
+        for a in range(2):
+            nc.scalar.activation(
+                out=w3_grouped[:, a * N * PACK : (a + 1) * N * PACK].rearrange("p (c j) -> p c j", j=PACK),
+                in_=w3_raw[a][:].rearrange("p j c -> p c j"),
+                func=COPY,
+                scale=-1.0,
+            )
+        w3_codes = kept([P, 2 * N], I32, "w3_codes")
+        w3_scales = kept([P, 2 * N], U8, "w3_scales")
+
+        for lo, hi in ((0, 512), (512, 2 * N)):
+            nc.vector.quantize_mx(
+                out=w3_codes[:, lo:hi].bitcast(FP8X4),
+                scales=w3_scales[:, lo:hi],
+                in_=w3_grouped[:, PACK * lo : PACK * hi],
+            )
+
+        for i, tag in ((2, "big_1"), (3, "w1_raw_10")):
+            pages.append(kept([P, T2], F32, "page_%d" % i, tag=tag, pool=late))
+            nc.gpsimd.memset(pages[-1][:], 0.0)
 
         x_rows_first = kept([P, PACK * S], F32, "x_first")
         x_first = [x_rows_first[:, i * S : (i + 1) * S] for i in range(PACK)]
@@ -209,9 +244,9 @@ def tile_list_arms_conflict_scores_kernel(
         for i in range(PACK):
             file_entries(h_second[i], i, 0, S)
 
-        def add_and_group(b, c, x_rows, dst):
+        def add_and_group(b, c, x_rows, dst, sum_bank, back_bank):
             cols = slice(c * BLOCK, (c + 1) * BLOCK)
-            z_t = psum.tile([P, PACK, P], F32, name="z_t", tag="z_t")
+            z_t = bank(sum_bank, [P, PACK, P], "z_t")
             for i in range(PACK):
                 nc.tensor.matmul(
                     z_t[:, i, :], tinct_sb[b][:, i, cols], identity[:], start=(i == 0), stop=False, is_transpose=True
@@ -225,7 +260,7 @@ def tile_list_arms_conflict_scores_kernel(
                 out=pairs[:].rearrange("j (u p e) -> j u p e", u=2, e=2),
                 in_=z_t[:].rearrange("j (u e) p -> j u p e", u=2),
             )
-            back = psum.tile([P, 2, BLOCK], F32, name="back", tag="back")
+            back = bank(back_bank, [P, 2, BLOCK], "back")
             for u in range(2):
                 nc.tensor.transpose(back[:, u, :], pairs[:].bitcast(F32)[:, u * P : (u + 1) * P], identity[:])
             nc.scalar.copy(
@@ -238,9 +273,8 @@ def tile_list_arms_conflict_scores_kernel(
             for c in range(4 * half, 4 * half + 4):
                 cols = slice(c * BLOCK, (c + 1) * BLOCK)
                 local = c - 4 * half
-                add_and_group(
-                    0, c, [x[:, cols] for x in x_first], grouped[:, local * PACK * BLOCK : (local + 1) * PACK * BLOCK]
-                )
+                dst = grouped[:, local * PACK * BLOCK : (local + 1) * PACK * BLOCK]
+                add_and_group(0, c, [x[:, cols] for x in x_first], dst, 2 + c % 2, 4 + c % 2)
         z0_codes = kept([P, S], I32, "z0_codes", tag="h_3")
         z0_scales = kept([P, S], U8, "z0_scales")
 
@@ -250,29 +284,9 @@ def tile_list_arms_conflict_scores_kernel(
                 out=z0_codes[:, cols].bitcast(FP8X4), scales=z0_scales[:, cols], in_=z0_grouped[half][:]
             )
 
-        w3_grouped = kept([P, 2 * N * PACK], BF16, "w3_grouped")
-        for a in range(2):
-            nc.scalar.activation(
-                out=w3_grouped[:, a * N * PACK : (a + 1) * N * PACK].rearrange("p (c j) -> p c j", j=PACK),
-                in_=w3_raw[a][:].rearrange("p j c -> p c j"),
-                func=COPY,
-                scale=-1.0,
-            )
-        w3_codes = kept([P, 2 * N], I32, "w3_codes", tag="h_2")
-        w3_scales = kept([P, 2 * N], U8, "w3_scales")
-
-        def quantize_w3():
-            for lo, hi in ((0, 512), (512, 2 * N)):
-                nc.vector.quantize_mx(
-                    out=w3_codes[:, lo:hi].bitcast(FP8X4),
-                    scales=w3_scales[:, lo:hi],
-                    in_=w3_grouped[:, PACK * lo : PACK * hi],
-                )
-
         def scores(c, z1_codes, z1_scales):
             cols = slice(c * BLOCK, (c + 1) * BLOCK)
-            tag = "h_bank" if c % 2 else "diff"
-            diff = psum.tile([P, N_TILES, BLOCK], F32, name="diff", tag=tag)
+            diff = bank((5, 6, 7, 0, 1, 2, 3, 5)[c], [P, N_TILES, BLOCK], "diff")
             for a in range(2):
                 for t in range(N_TILES):
                     w_cols = slice(a * N + t * P, a * N + (t + 1) * P)
@@ -281,7 +295,7 @@ def tile_list_arms_conflict_scores_kernel(
                         lhsT=w3_codes[:, w_cols].bitcast(FP8X4),
                         lhsT_scale=w3_scales[:, w_cols],
                         rhs=v_codes[a][:, cols].bitcast(FP8X4),
-                        rhs_scale=v_scales[4 * a : P, cols],
+                        rhs_scale=v_scales[a][:, cols],
                         start=(a == 0 and t == 0),
                         stop=False,
                     )
@@ -305,24 +319,23 @@ def tile_list_arms_conflict_scores_kernel(
         for step in range(BLOCKS + LAG):
             if step < BLOCKS:
                 c = step
-                slot = "late_%d" % (c % (LAG + 1))
+                slot = "late_%d" % (c % ROUTED)
                 x = kept([P, PACK, BLOCK], F32, "x_late_%d" % c, tag=slot)
                 for i in range(PACK):
                     read_entries(x[:, i, :], i, c * BLOCK, BLOCK)
-                if c in DIRECT_BLOCKS:
-                    grouped = kept([P, PACK * BLOCK], BF16, "z1_direct_%d" % c)
-                    rounded = kept([P, PACK, BLOCK], BF16, "z1_rounded_%d" % c)
+                if c < ROUTED:
+                    grouped = kept([P, PACK * BLOCK], BF16, "z1_grouped_%d" % c, tag=slot)
+                    add_and_group(1, c, [x[:, i, :] for i in range(PACK)], grouped[:], c, 4)
+                else:
+                    rounded = kept([P, PACK, BLOCK], BF16, "z1_rounded_%d" % c, tag="z1_grouped_%d" % (c - LAG))
                     nc.vector.tensor_tensor(rounded[:], x[:], tinct_sb[1][:, :, c * BLOCK : (c + 1) * BLOCK], ADD)
+                    grouped = kept([P, PACK * BLOCK], BF16, "z1_grouped_%d" % c)
                     copy_call = nc.vector.tensor_copy if c == BLOCKS - 1 else nc.scalar.copy
                     copy_call(
                         out=grouped[:].rearrange("p (j i) -> p j i", i=PACK), in_=rounded[:].rearrange("p i j -> p j i")
                     )
-                else:
-                    grouped = kept([P, PACK * BLOCK], BF16, "z1_grouped_%d" % c, tag=slot)
-                    add_and_group(1, c, [x[:, i, :] for i in range(PACK)], grouped[:])
                 z1_grouped.append(grouped)
             if step == 1:
-                quantize_w3()
                 quantize_z0(0)
             if step == 3:
                 quantize_z0(1)

from contextlib import ExitStack

import concourse.mybir as mybir
from concourse.masks import make_identity

T, S, T2, K, H, N = 4096, 1024, 2048, 1024, 1024, 384
FLOPS = 2 * S * (K * H + H * N + K * N)

F32 = mybir.dt.float32
BF16 = mybir.dt.bfloat16
I32 = mybir.dt.int32
U32 = mybir.dt.uint32
U16 = mybir.dt.uint16
U8 = mybir.dt.uint8
FP8X4 = mybir.dt.float8_e4m3fn_x4
FP4X4 = mybir.dt.float4_e2m1fn_x4
MULT = mybir.AluOpType.mult
ADD = mybir.AluOpType.add
COPY = mybir.ActivationFunctionType.Copy
SQUARE = mybir.ActivationFunctionType.Square

P = 128
PACK = 4
K_PASS = P * PACK
BANK = 512
BLOCK = 128
N_TILES = N // P
BLOCKS = S // BLOCK
LAG = 2
ROUTED = 4


def tile_list_arms_conflict_scores_kernel(
    tc, tab_words, tab_scales, offs, offs2, offs3, w1, gain, wgs, wgt, tinct, w3, w4_words, w4_scales, out
):
    nc = tc.nc

    def entries(first, count):
        return slice(first // 16, (first + count) // 16)

    with ExitStack() as ctx:
        lists = ctx.enter_context(tc.tile_pool(name="lists", bufs=1))
        keep = ctx.enter_context(tc.tile_pool(name="keep", bufs=1))
        ring = ctx.enter_context(tc.tile_pool(name="ring", bufs=3))
        psum = ctx.enter_context(tc.psum_pool(name="psum", bufs=1))

        idx = lists.tile([P, S // 16], U16, name="idx")
        idx2 = lists.tile([P, S // 16], U16, name="idx2")
        idx3 = lists.tile([P, S // 16], U16, name="idx3")

        def kept(shape, dtype, name, tag=None, pool=keep):
            return pool.tile(shape, dtype, name=name, tag=tag or name, align_bytes=64)

        def bank(n, shape, name):
            return psum.tile(shape, F32, name=name, tag="bank_%d" % n)

        def load_w1(b, a, pool):
            raw = kept([P, PACK, K_PASS], F32, "w1_raw_%d%d" % (b, a), pool=pool)
            rows = w1[a * K_PASS : (a + 1) * K_PASS, b * K_PASS : (b + 1) * K_PASS]
            nc.sync.dma_start(out=raw[:], in_=rows.rearrange("(p j) c -> p j c", j=PACK))
            return raw

        def group_w1(copy_call, raw, dst):
            copy_call(
                out=dst.rearrange("p (t m j) -> p t m j", t=PACK, j=PACK),
                in_=raw[:].rearrange("p j (m t) -> p t m j", t=PACK),
            )

        def load_words(a, pool):
            table = kept([P, T], I32, "table_%d" % a, tag="big_%d" % a, pool=pool)
            nc.sync.dma_start(out=table[:], in_=tab_words[a].rearrange("p t i -> p (t i)").bitcast(I32))
            return table

        picked_rows = kept([P, S], U8, "picked_rows")
        v_scales = [kept([P, S], U8, "v_scales_%d" % a) for a in range(2)]
        with tc.tile_pool(name="scale_stage", bufs=1) as scale_stage:
            scale_rows = kept([P, T], U8, "scale_rows", pool=scale_stage)
            nc.sync.dma_start(
                out=scale_rows[0:32, :].bitcast(I32), in_=tab_scales.rearrange("a q t -> (a q) t").bitcast(I32)
            )
            nc.gpsimd.memset(scale_rows[32:64, :].bitcast(I32), 0)
            nc.gpsimd.memset(scale_rows[64:128, :].bitcast(I32), 0)
            for plane in v_scales:
                nc.vector.memset(plane[:].bitcast(I32), 0)
            nc.sync.dma_start(idx[:], offs)
            words = [load_words(0, keep)]
            nc.sync.dma_start(idx2[:], offs2)
            nc.sync.dma_start(idx3[:], offs3)
            w1_raw = [load_w1(0, a, keep) for a in range(2)]
            nc.vector.tensor_copy(picked_rows[:], scale_rows[:].indirect(idx[:]))
        late = ctx.enter_context(tc.tile_pool(name="late", bufs=1))

        def place_scale_rows(a):
            for q in range(4):
                nc.sync.dma_start(
                    out=v_scales[a][32 * q : 32 * q + 4, :].bitcast(I32),
                    in_=picked_rows[16 * a + 4 * q : 16 * a + 4 * q + 4, :].bitcast(I32),
                )

        place_scale_rows(0)
        words.append(load_words(1, late))
        place_scale_rows(1)
        gains = kept([P, 2 * PACK], F32, "gains", pool=late)
        nc.sync.dma_start(
            out=gains[:].rearrange("p (b i) -> p b i", b=2), in_=gain.rearrange("(b p i) -> p b i", b=2, i=PACK)
        )
        wgs_sb = kept([P, S], F32, "wgs_sb", pool=late)
        nc.sync.dma_start(out=wgs_sb[:], in_=wgs)
        wgt_sb = kept([P, S], F32, "wgt_sb", pool=late)
        nc.sync.dma_start(out=wgt_sb[:], in_=wgt)

        v_codes = [kept([P, S], I32, "v_codes_0")]
        nc.vector.tensor_copy(v_codes[0][:].bitcast(U32), words[0][:].bitcast(U32).indirect(idx[:]))

        pages = [kept([P, T2], F32, "page_%d" % i) for i in range(2)]
        nc.vector.memset(pages[0][:], 0.0)
        nc.gpsimd.memset(pages[1][:], 0.0)

        identity = kept([P, P], F32, "identity")
        make_identity(nc, identity[:])

        w1_codes = [kept([P, 2 * K_PASS], I32, "w1_codes_%d" % b) for b in range(2)]
        early_planes = kept([P, K_PASS], U8, "w1_early_planes")
        late_planes = kept([P, 2 * K_PASS], U8, "w1_late_planes")
        w1_planes = [
            [early_planes[4 * a : P, :] for a in range(2)],
            [late_planes[:, a * K_PASS : (a + 1) * K_PASS] for a in range(2)],
        ]
        for a in range(2):
            grouped = kept([P, PACK * K_PASS], BF16, "w1_grouped_%d" % a, tag="w1_grouped_%d" % a, pool=(keep, late)[a])
            group_w1((nc.scalar.copy, nc.vector.tensor_copy)[a], w1_raw[a], grouped[:])
            cols = slice(a * K_PASS, (a + 1) * K_PASS)
            nc.vector.quantize_mx(out=w1_codes[0][:, cols].bitcast(FP8X4), scales=w1_planes[0][a], in_=grouped[:])

        v_codes.append(kept([P, S], I32, "v_codes_1", tag="w1_grouped_1", pool=late))
        for first in range(0, S, BANK):
            nc.vector.tensor_copy(
                v_codes[1][:, first : first + BANK].bitcast(U32),
                words[1][:].bitcast(U32).indirect(idx[:, entries(first, BANK)]),
            )

        def features(b, i):
            h = kept([P, S], F32, "h_%d%d" % (b, i), tag="h_%d" % i)
            banks = [bank(half, [P, BANK], "h_bank") for half in range(2)]
            for a in range(2):
                w_cols = slice(a * K_PASS + i * P, a * K_PASS + (i + 1) * P)
                for half in range(2):
                    cols = slice(half * BANK, (half + 1) * BANK)
                    nc.tensor.matmul_mx(
                        out=banks[half][:],
                        lhsT=w1_codes[b][:, w_cols].bitcast(FP8X4),
                        lhsT_scale=w1_planes[b][a][:, i * P : (i + 1) * P],
                        rhs=v_codes[a][:, cols].bitcast(FP8X4),
                        rhs_scale=v_scales[a][:, cols],
                        start=(a == 0),
                        stop=(a == 1),
                    )
            for half in range(2):
                cols = slice(half * BANK, (half + 1) * BANK)
                nc.scalar.activation(
                    out=h[:, cols], in_=banks[half][:], func=COPY, scale=gains[:, PACK * b + i : PACK * b + i + 1]
                )
            return h

        def file_entries(h, i, first, count):
            cols = slice(first, first + count)
            nc.vector.tensor_tensor(
                pages[i][:].indirect(idx2[:, entries(first, count)]), h[:, cols], wgs_sb[:, cols], MULT
            )

        def read_entries(x, i, first, count):
            nc.vector.tensor_tensor(
                x, pages[i][:].indirect(idx3[:, entries(first, count)]), wgt_sb[:, first : first + count], MULT
            )

        h_first = [features(0, i) for i in range(PACK)]

        w1_raw = [load_w1(1, a, late) for a in range(2)]
        tinct_sb = [kept([P, PACK, S], F32, "tinct_0", tag="big_0"), kept([P, PACK, S], F32, "tinct_1", pool=late)]

        def load_tinct(b):
            nc.sync.dma_start(
                out=tinct_sb[b][:], in_=tinct[b * K_PASS : (b + 1) * K_PASS, :].rearrange("(p i) j -> p i j", i=PACK)
            )

        w3_raw = []
        for a in range(2):
            raw = kept([P, PACK, N], F32, "w3_raw_%d" % a, pool=late)
            nc.sync.dma_start(
                out=raw[:], in_=w3[a * K_PASS : (a + 1) * K_PASS, :].rearrange("(p j) c -> p j c", j=PACK)
            )
            w3_raw.append(raw)
        load_tinct(0)
        w4_codes = kept([P, 2, 2 * N], U8, "w4_codes", pool=late)
        nc.sync.dma_start(out=w4_codes[:].bitcast(I32), in_=w4_words.rearrange("a p n -> p a n").bitcast(I32))
        w4_planes = kept([P, 2, N], U8, "w4_planes", pool=late)
        nc.vector.memset(w4_planes[:].bitcast(I32), 0)
        for q in range(4):
            nc.sync.dma_start(
                out=w4_planes[32 * q : 32 * q + 4].bitcast(I32),
                in_=w4_scales[:, 4 * q : 4 * q + 4, :].rearrange("a r n -> r a n").bitcast(I32),
            )
        load_tinct(1)

        late_grouped = kept([P, 2 * PACK * (K_PASS + N)], BF16, "late_grouped", tag="x_first")
        for a in range(2):
            group_w1(nc.scalar.copy, w1_raw[a], late_grouped[:, a * PACK * K_PASS : (a + 1) * PACK * K_PASS])
        nc.vector.quantize_mx(
            out=w1_codes[1][:].bitcast(FP8X4), scales=late_planes[:], in_=late_grouped[:, 0 : 2 * PACK * K_PASS]
        )

        w3_grouped = late_grouped[:, 2 * PACK * K_PASS :]
        for a in range(2):
            nc.scalar.activation(
                out=w3_grouped[:, a * N * PACK : (a + 1) * N * PACK].rearrange("p (c j) -> p c j", j=PACK),
                in_=w3_raw[a][:].rearrange("p j c -> p c j"),
                func=COPY,
                scale=-1.0,
            )
        w3_codes = kept([P, 2 * N], I32, "w3_codes")
        w3_scales = kept([P, 2 * N], U8, "w3_scales")

        for lo, hi in ((0, 512), (512, 2 * N)):
            nc.vector.quantize_mx(
                out=w3_codes[:, lo:hi].bitcast(FP8X4),
                scales=w3_scales[:, lo:hi],
                in_=w3_grouped[:, PACK * lo : PACK * hi],
            )

        for i, tag in ((2, "big_1"), (3, "w1_raw_10")):
            pages.append(kept([P, T2], F32, "page_%d" % i, tag=tag, pool=late))
            nc.gpsimd.memset(pages[-1][:], 0.0)

        x_rows_first = kept([P, PACK * S], F32, "x_first")
        x_first = [x_rows_first[:, i * S : (i + 1) * S] for i in range(PACK)]
        for first in range(0, S, BANK):
            file_entries(h_first[0], 0, first, BANK)
        for i in range(1, PACK):
            file_entries(h_first[i], i, 0, S)
        for i in range(PACK):
            read_entries(x_first[i], i, 0, S)

        h_second = [features(1, i) for i in range(PACK)]
        for i in range(PACK):
            file_entries(h_second[i], i, 0, S)

        def add_and_group(b, c, x_rows, dst, sum_bank, back_bank):
            cols = slice(c * BLOCK, (c + 1) * BLOCK)
            z_t = bank(sum_bank, [P, PACK, P], "z_t")
            for i in range(PACK):
                nc.tensor.matmul(
                    z_t[:, i, :], tinct_sb[b][:, i, cols], identity[:], start=(i == 0), stop=False, is_transpose=True
                )
            for i in range(PACK):
                nc.tensor.matmul(
                    z_t[:, i, :], x_rows[i], identity[:], start=False, stop=(i == PACK - 1), is_transpose=True
                )
            pairs = ring.tile([P, PACK * P], BF16, name="pairs", tag="pairs", align_bytes=64)
            nc.scalar.copy(
                out=pairs[:].rearrange("j (u p e) -> j u p e", u=2, e=2),
                in_=z_t[:].rearrange("j (u e) p -> j u p e", u=2),
            )
            back = bank(back_bank, [P, 2, BLOCK], "back")
            for u in range(2):
                nc.tensor.transpose(back[:, u, :], pairs[:].bitcast(F32)[:, u * P : (u + 1) * P], identity[:])
            nc.scalar.copy(
                out=dst.bitcast(F32).rearrange("p (j u) -> p j u", u=2), in_=back[:].rearrange("p u j -> p j u")
            )

        z0_grouped = [kept([P, PACK * BANK], BF16, "z0_grouped_%d" % half) for half in range(2)]
        for half in range(2):
            grouped = z0_grouped[half]
            for c in range(4 * half, 4 * half + 4):
                cols = slice(c * BLOCK, (c + 1) * BLOCK)
                local = c - 4 * half
                dst = grouped[:, local * PACK * BLOCK : (local + 1) * PACK * BLOCK]
                add_and_group(0, c, [x[:, cols] for x in x_first], dst, 2 + c % 2, 4 + c % 2)
        z0_codes = kept([P, S], I32, "z0_codes", tag="h_3")
        z0_scales = kept([P, S], U8, "z0_scales")

        def quantize_z0(half):
            cols = slice(half * BANK, (half + 1) * BANK)
            nc.vector.quantize_mx(
                out=z0_codes[:, cols].bitcast(FP8X4), scales=z0_scales[:, cols], in_=z0_grouped[half][:]
            )

        def scores(c, z1_codes, z1_scales):
            cols = slice(c * BLOCK, (c + 1) * BLOCK)
            diff = bank((5, 6, 7, 0, 1, 2, 3, 5)[c], [P, N_TILES, BLOCK], "diff")
            for a in range(2):
                for t in range(N_TILES):
                    w_cols = slice(a * N + t * P, a * N + (t + 1) * P)
                    nc.tensor.matmul_mx(
                        out=diff[:, t, :],
                        lhsT=w3_codes[:, w_cols].bitcast(FP8X4),
                        lhsT_scale=w3_scales[:, w_cols],
                        rhs=v_codes[a][:, cols].bitcast(FP8X4),
                        rhs_scale=v_scales[a][:, cols],
                        start=(a == 0 and t == 0),
                        stop=False,
                    )
            z_parts = [(z0_codes[:, cols], z0_scales[:, cols]), (z1_codes[:], z1_scales[:])]
            for b in range(2):
                for t in range(N_TILES):
                    nc.tensor.matmul_mx(
                        out=diff[:, t, :],
                        lhsT=w4_codes[:, b, 2 * t * P : 2 * (t + 1) * P].bitcast(FP4X4),
                        lhsT_scale=w4_planes[:, b, t * P : (t + 1) * P],
                        rhs=z_parts[b][0].bitcast(FP8X4),
                        rhs_scale=z_parts[b][1],
                        start=False,
                        stop=(b == 1 and t == N_TILES - 1),
                    )
            squared = ring.tile([P, N_TILES, BLOCK], F32, name="squared", tag="squared")
            nc.scalar.activation(out=squared[:], in_=diff[:], func=SQUARE)
            nc.sync.dma_start(out=out[:, cols].rearrange("(t p) j -> p t j", p=P), in_=squared[:])

        z1_grouped = []
        for step in range(BLOCKS + LAG):
            if step < BLOCKS:
                c = step
                slot = "late_%d" % (c % ROUTED)
                x = kept([P, PACK, BLOCK], F32, "x_late_%d" % c, tag=slot)
                for i in range(PACK):
                    read_entries(x[:, i, :], i, c * BLOCK, BLOCK)
                if c < ROUTED:
                    grouped = kept([P, PACK * BLOCK], BF16, "z1_grouped_%d" % c, tag=slot)
                    add_and_group(1, c, [x[:, i, :] for i in range(PACK)], grouped[:], c, 4)
                else:
                    rounded = kept([P, PACK, BLOCK], BF16, "z1_rounded_%d" % c, tag="z1_grouped_%d" % (c - LAG))
                    nc.vector.tensor_tensor(rounded[:], x[:], tinct_sb[1][:, :, c * BLOCK : (c + 1) * BLOCK], ADD)
                    grouped = kept([P, PACK * BLOCK], BF16, "z1_grouped_%d" % c)
                    copy_call = nc.vector.tensor_copy if c == BLOCKS - 1 else nc.scalar.copy
                    copy_call(
                        out=grouped[:].rearrange("p (j i) -> p j i", i=PACK), in_=rounded[:].rearrange("p i j -> p j i")
                    )
                z1_grouped.append(grouped)
            if step == 1:
                quantize_z0(0)
            if step == 3:
                quantize_z0(1)
            if step >= LAG:
                c = step - LAG
                z1_codes = ring.tile([P, BLOCK], I32, name="z1_codes", tag="z1_codes", align_bytes=64)
                z1_scales = ring.tile([P, BLOCK], U8, name="z1_scales", tag="z1_scales", align_bytes=64)
                nc.vector.quantize_mx(out=z1_codes[:].bitcast(FP8X4), scales=z1_scales[:], in_=z1_grouped[c][:])
                scores(c, z1_codes, z1_scales)
